import numpy as np
import ml_dtypes


def mxq(x, axis, fmt="e4m3"):
    dtype, down = {"e4m3": (ml_dtypes.float8_e4m3fn, 7), "e5m2": (ml_dtypes.float8_e5m2, 14)}[fmt]
    v = np.moveaxis(np.asarray(x, np.float32).astype(ml_dtypes.bfloat16).astype(np.float64), axis, -1)
    blocks = v.reshape(v.shape[:-1] + (-1, 32))
    amax = np.abs(blocks).max(-1, keepdims=True)
    byte = np.maximum(np.where(amax > 0, np.frexp(amax)[1] - 1 + 127, 0) - down, 1)
    scale = np.exp2(byte - 127.0)
    codes = (blocks / scale).astype(np.float32).astype(dtype).astype(np.float64)
    return np.moveaxis((codes * scale).reshape(v.shape), -1, axis)


WIDE = False


def mx_kscale(k):
    if not WIDE:
        return np.ones(k)
    levels = np.array([10, -10, 5, -5, 0])
    if k % 512:
        return np.exp2(np.random.permutation(np.resize(levels, k // 32))).repeat(32)
    a = np.empty((k // 512, 16))
    for p in range(k // 512):
        a[p, :8] = np.random.permutation(np.resize(levels, 8))
        for g in range(8):
            far = levels[np.abs(levels - a[p, g]) >= 10]
            a[p, g + 8] = far[np.random.randint(len(far))]
    return np.exp2(a.ravel()).repeat(32)


def f64(x):
    return np.asarray(x).astype(np.float64)


def striped(idx):
    return np.tile(idx.reshape(-1, 16).T, (8, 1)).astype(np.uint16)


def unstriped(offs):
    return offs[:16].T.reshape(-1).astype(np.int64)


def striped8(idx):
    return np.concatenate([x.reshape(-1, 16).T for x in idx]).astype(np.uint16)


def runs(offs, k):
    lists = np.stack([offs[16 * r : 16 * r + 16].T.reshape(-1) for r in range(8)]).astype(np.int64)
    return lists[np.arange(k) % 512 // 64]


def pack_weight(w):
    k, n = w.shape
    w = f64(np.asarray(w, np.float32).astype(ml_dtypes.bfloat16)).reshape(k // 32, 32, n)
    amax = np.abs(w).max(1)
    byte = np.clip(np.where(amax > 0, np.frexp(amax)[1] - 1 + 127 - 7, 1), 1, 254)
    scaled = (w * np.exp2(127.0 - byte)[:, None, :]).reshape(k, n).astype(np.float32)
    words = np.ascontiguousarray(scaled.reshape(k // 512, 128, 4, n).transpose(0, 1, 3, 2)).astype(ml_dtypes.float8_e4m3fn).view(np.uint8)
    return words, np.ascontiguousarray(byte.astype(np.uint8).reshape(k // 512, 16, n))


def unpack_weight(words, scales):
    g, p, n, _ = words.shape
    vals = np.ascontiguousarray(words).view(ml_dtypes.float8_e4m3fn).astype(np.float64) * np.repeat(np.exp2(scales.astype(np.float64) - 127.0), 8, axis=1)[..., None]
    return vals.transpose(0, 1, 3, 2).reshape(g * 512, n)


E2M1 = np.array([0.0, 0.5, 1.0, 1.5, 2.0, 3.0, 4.0, 6.0, -0.0, -0.5, -1.0, -1.5, -2.0, -3.0, -4.0, -6.0])


def pack_fp4(w):
    k, n = w.shape
    w = f64(np.asarray(w, np.float32).astype(ml_dtypes.bfloat16)).reshape(k // 32, 32, n)
    amax = np.abs(w).max(1)
    mant, ex = np.frexp(amax / 6.0)
    byte = np.clip(np.where(amax > 0, np.where(mant > 0.5, ex, ex - 1) + 127, 1), 1, 254)
    scaled = (w * np.exp2(127.0 - byte)[:, None, :]).reshape(k, n).astype(np.float32)
    c = np.ascontiguousarray(scaled.reshape(k // 512, 128, 4, n).transpose(0, 1, 3, 2)).astype(ml_dtypes.float4_e2m1fn).view(np.uint8) & 0xF
    words = (c[..., 0::2] | (c[..., 1::2] << 4)).reshape(k // 512, 128, 2 * n)
    return np.ascontiguousarray(words), np.ascontiguousarray(byte.astype(np.uint8).reshape(k // 512, 16, n))


def unpack_fp4(words, scales):
    g, _, n = scales.shape
    words = np.ascontiguousarray(words).reshape(g, 128, n, 2)
    nib = np.empty((g, 128, n, 4), np.uint8)
    nib[..., 0::2] = words & 0xF
    nib[..., 1::2] = words >> 4
    vals = E2M1[nib] * np.repeat(np.exp2(scales.astype(np.float64) - 127.0), 8, axis=1)[..., None]
    return vals.transpose(0, 1, 3, 2).reshape(g * 512, n)


def planes(y):
    n, m = y.shape
    v = y.astype(np.float32).astype(ml_dtypes.bfloat16).astype(np.float64).reshape(n // 32, 32, m)
    top = np.abs(v).max(1)
    byte = np.clip(np.where(top > 0, np.frexp(top)[1] - 1 + 127 - 7, 1), 1, 254)
    codes = (v * np.exp2(127.0 - byte)[:, None, :]).reshape(n, m).astype(np.float32).astype(ml_dtypes.float8_e4m3fn).view(np.uint8)
    words = codes.reshape(n // 512, 128, 4, m).transpose(0, 1, 3, 2)
    return np.ascontiguousarray(words), np.ascontiguousarray(byte.astype(np.uint8).reshape(n // 512, 16, m))


K, T, S, V, H = 512, 2048, 512, 512, 512


def setup_inputs():
    n = np.random.standard_normal
    s = mx_kscale(K)[:, None]
    u = mx_kscale(S)
    packed_xT = pack_weight(n((K, T)) * s)
    packed_w1 = pack_fp4(n((K, H)) / np.sqrt(K) / s)
    packed_w2 = pack_fp4(n((K, H)) / np.sqrt(K) / s)
    return {
        "x_words": packed_xT[0],
        "x_scales": packed_xT[1],
        "w1_words": packed_w1[0],
        "w1_scales": packed_w1[1],
        "w2_words": packed_w2[0],
        "w2_scales": packed_w2[1],
        "ga": (np.random.uniform(0.5, 1.5, (H, 1)) * u[:, None]).astype(np.float32),
        "gb": (np.random.uniform(0.5, 1.5, (H, 1)) / u[:, None]).astype(np.float32),
        "offs": striped(np.random.permutation(T)[:S]),
        "two": striped(np.random.permutation(T)[:V]),
        "n1": striped8(np.stack([np.random.permutation(S) for _ in range(8)])),
        "n2": striped8(np.stack([np.random.permutation(S) for _ in range(8)])),
        "n3": striped8(np.stack([np.random.permutation(V) for _ in range(8)])),
        "n4": striped8(np.stack([np.random.permutation(V) for _ in range(8)])),
        "n5": striped8(np.stack([np.random.permutation(V) for _ in range(8)])),
        "n6": striped8(np.stack([np.random.permutation(V) for _ in range(8)])),
    }


def reference(x_words, x_scales, w1_words, w1_scales, w2_words, w2_scales, ga, gb, offs, two, n1, n2, n3, n4, n5, n6):
    xq = unpack_weight(x_words, x_scales)[:, unstriped(offs)]
    a = unpack_fp4(w1_words, w1_scales).T @ xq
    st = a + a[np.arange(H)[:, None], runs(n1, H)]
    z = f64(ga) * (st * (np.tanh(st[np.arange(H)[:, None], runs(n2, H)])))
    x_two = unpack_weight(x_words, x_scales)[:, unstriped(two)]
    b = unpack_fp4(w2_words, w2_scales).T @ x_two
    z2 = f64(gb) * (0.75 * (b[np.arange(H)[:, None], runs(n3, H)] + b[np.arange(H)[:, None], runs(n4, H)]) - b)
    s = 0.0625 * ((mxq(z, 0, "e4m3").T @ mxq(z2, 0, "e4m3")))
    st2 = np.maximum(s, s[np.arange(S)[:, None], runs(n5, S)])
    out_0 = st2[np.arange(S)[:, None], runs(n6, S)] - (0.5 * s)
    return (out_0,) + planes(out_0)

@@ -1,0 +1,248 @@
+from contextlib import ExitStack
+
+import concourse.mybir as mybir
+from concourse.masks import make_identity
+
+F32 = mybir.dt.float32
+BF16 = mybir.dt.bfloat16
+I32 = mybir.dt.int32
+U32 = mybir.dt.uint32
+U16 = mybir.dt.uint16
+U8 = mybir.dt.uint8
+FP8X4 = mybir.dt.float8_e4m3fn_x4
+FP4X4 = mybir.dt.float4_e2m1fn_x4
+ALU = mybir.AluOpType
+ACT = mybir.ActivationFunctionType
+
+P = 128
+T = 2048
+N = 512
+PACK = 4
+HALVES = ((0, 256), (256, 512))
+TAPER = ((0, 256), (256, 384), (384, 512))
+FLOPS = 3 * 2 * 512 * 512 * 512
+
+
+def tile_picked_kqhopplaphopb_none_po_kernel(
+    tc, x_words, x_scales, w1_words, w1_scales, w2_words, w2_scales, ga, gb, offs, two, n1, n2, n3, n4, n5, n6, out_0, out_1, out_2
+):
+    nc = tc.nc
+    with ExitStack() as ctx:
+        lists = ctx.enter_context(tc.tile_pool(name="lists", bufs=1))
+        sb = ctx.enter_context(tc.tile_pool(name="sb", bufs=1))
+        ps = ctx.enter_context(tc.psum_pool(name="ps", bufs=1))
+
+        def load_list(name, src):
+            tile = lists.tile([P, N // 16], U16, name=name)
+            nc.sync.dma_start(tile[:], src)
+            return tile
+
+        def entries(tile, lo, hi):
+            return tile[:, lo // 16 : hi // 16]
+
+        def load_scales(queue, tile, src):
+            for q in range(4):
+                queue.dma_start(tile[32 * q : 32 * q + 4, :].bitcast(I32), src[0, 4 * q : 4 * q + 4, :].bitcast(I32))
+
+        def bank(k, name):
+            return ps.tile([P, N], F32, name=name, tag="bank%d" % k)
+
+        xs = sb.tile([P, T], U8, name="xs")
+        w1s_raw = sb.tile([P, N], U8, name="w1s_raw")
+        w2s_raw = sb.tile([P, N], U8, name="w2s_raw")
+        g_rows = sb.tile([P, P], F32, name="g_rows")
+        nc.vector.memset(xs[:].bitcast(I32), 0)
+        nc.vector.memset(w1s_raw[:].bitcast(I32), 0)
+        nc.gpsimd.memset(w2s_raw[:].bitcast(I32), 0)
+        nc.gpsimd.memset(g_rows[:], 0.0)
+        ident = sb.tile([P, P], F32, name="ident")
+        make_identity(nc, ident[:])
+
+        offs_t = load_list("offs_t", offs)
+        two_t = load_list("two_t", two)
+        load_scales(nc.sync, xs, x_scales)
+        xw = sb.tile([P, T], I32, name="xw")
+        nc.sync.dma_start(xw[:], x_words[0].rearrange("p n t -> p (n t)").bitcast(I32))
+        w1w_raw = sb.tile([P, 256], I32, name="w1w_raw")
+        w2w_raw = sb.tile([P, 256], I32, name="w2w_raw")
+        nc.scalar.dma_start(w1w_raw[:], w1_words[0].bitcast(I32))
+        load_scales(nc.scalar, w1s_raw, w1_scales)
+        n1_t = load_list("n1_t", n1)
+        for r, g in ((0, ga), (4, gb)):
+            nc.sync.dma_start(
+                g_rows[r : r + 4, :].rearrange("t (b q) -> t b q", q=8),
+                g.rearrange("(b t q) o -> t b (q o)", t=4, q=8),
+            )
+        nc.sync.dma_start(w2w_raw[:], w2_words[0].bitcast(I32))
+        load_scales(nc.sync, w2s_raw, w2_scales)
+        n2_t = load_list("n2_t", n2)
+        n3_t = load_list("n3_t", n3)
+        n4_t = load_list("n4_t", n4)
+        n5_t = load_list("n5_t", n5)
+        n6_t = load_list("n6_t", n6)
+
+        def deal(name, words_raw, scales_raw):
+            words = sb.tile([P, 2 * N], U8, name=name + "w", align_bytes=64)
+            scales = sb.tile([P, N], U8, name=name + "s", align_bytes=64)
+            nc.vector.tensor_copy(
+                words[:].bitcast(I32).rearrange("p (t b q) -> p t b q", t=4, q=4),
+                words_raw[:].rearrange("p (b t q) -> p t b q", t=4, q=4),
+            )
+            nc.vector.tensor_copy(
+                scales[:].bitcast(I32).rearrange("p (t b q) -> p t b q", t=4, q=2),
+                scales_raw[:].bitcast(I32).rearrange("p (b t q) -> p t b q", t=4, q=2),
+            )
+            return words, scales
+
+        def pick_scales(name, lst):
+            tile = sb.tile([P, N], U8, name=name, align_bytes=64)
+            nc.vector.tensor_copy(tile[:], xs[:].indirect(lst[:]))
+            return tile
+
+        def pick_words(name, lst):
+            tile = sb.tile([P, N], U32, name=name, align_bytes=64)
+            nc.vector.tensor_copy(tile[:], xw[:].bitcast(U32).indirect(lst[:]))
+            return tile
+
+        def project(dst, w, t, words, scales):
+            nc.tensor.matmul_mx(
+                out=dst[:],
+                lhsT=w[0][:, 256 * t : 256 * (t + 1)].bitcast(FP4X4),
+                lhsT_scale=w[1][:, P * t : P * (t + 1)],
+                rhs=words[:].bitcast(FP8X4),
+                rhs_scale=scales[:],
+                start=True,
+                stop=True,
+            )
+
+        xa_s = pick_scales("xa_s", offs_t)
+        xb_s = pick_scales("xb_s", two_t)
+        w1 = deal("w1", w1w_raw, w1s_raw)
+        xa_w = pick_words("xa_w", offs_t)
+        xb_w = pick_words("xb_w", two_t)
+        w2 = deal("w2", w2w_raw, w2s_raw)
+
+        g_ps = bank(7, "g_ps")
+        nc.tensor.transpose(g_ps[:, 0:P], g_rows[:], ident[:])
+        g_col = sb.tile([P, 12], F32, name="g_col")
+        nc.scalar.activation(g_col[:, 0:4], g_ps[:, 0:4], ACT.Copy)
+        nc.scalar.activation(g_col[:, 4:8], g_ps[:, 4:8], ACT.Copy, scale=0.75)
+        nc.scalar.activation(g_col[:, 8:12], g_ps[:, 4:8], ACT.Copy, scale=-1.0)
+
+        def planes(name, width=N):
+            return [sb.tile([P, width], F32, name="%s%d" % (name, t)) for t in range(PACK)]
+
+        a_win, a_own, st, th, gs = planes("a_win"), planes("a_own"), planes("st"), planes("th"), planes("gs")
+        b_win, b_neg = planes("b_win"), planes("b_neg")
+
+        a_ps = [bank(t, "a_ps%d" % t) for t in range(PACK)]
+        for t in range(PACK):
+            project(a_ps[t], w1, t, xa_w, xa_s)
+        b_ps = [bank(4 + t, "b_ps%d" % t) for t in range(PACK)]
+        for t in range(PACK):
+            project(b_ps[t], w2, t, xb_w, xb_s)
+
+        for t in range(PACK):
+            nc.scalar.copy(a_win[t][:], a_ps[t][:])
+            nc.scalar.copy(a_own[t][:], a_ps[t][:])
+            for lo, hi in HALVES:
+                nc.vector.tensor_tensor(st[t][:, lo:hi], a_win[t][:].indirect(entries(n1_t, lo, hi)), a_own[t][:, lo:hi], ALU.add)
+        z = sb.tile([P, PACK, N], F32, name="z")
+        for t in range(PACK):
+            nc.scalar.activation(th[t][:], st[t][:], ACT.Tanh)
+            nc.scalar.activation(gs[t][:], st[t][:], ACT.Copy, scale=g_col[:, t : t + 1])
+            for lo, hi in HALVES:
+                nc.vector.tensor_tensor(z[:, t, lo:hi], th[t][:].indirect(entries(n2_t, lo, hi)), gs[t][:, lo:hi], ALU.mult)
+        for t in range(PACK):
+            nc.scalar.activation(b_win[t][:], b_ps[t][:], ACT.Copy, scale=g_col[:, 4 + t : 5 + t])
+            nc.scalar.activation(b_neg[t][:], b_ps[t][:], ACT.Copy, scale=g_col[:, 8 + t : 9 + t])
+
+        z_bf = sb.tile([P, PACK, P, PACK], BF16, name="z_bf", align_bytes=64)
+        for lo, hi in HALVES:
+            nc.scalar.copy(
+                z_bf[:, :, lo // 4 : hi // 4, :].rearrange("p u m t -> p m t u"),
+                z[:, :, lo:hi].rearrange("p t (m u) -> p m t u", u=4),
+            )
+        z_w = sb.tile([P, N], U32, name="z_w", align_bytes=64)
+        z_s = sb.tile([P, N], U8, name="z_s", align_bytes=64)
+
+        def weave(engine_copy, name, src, width):
+            dst = sb.tile([P, width, PACK], BF16, name=name, align_bytes=64)
+            engine_copy(dst[:].rearrange("p (c i) t -> p c t i", i=4), src[:].rearrange("p t (c i) -> p c t i", i=4))
+            return dst
+
+        def quantize(words, scales, src):
+            nc.vector.quantize_mx(out=words.bitcast(FP8X4), scales=scales, in_=src)
+
+        z2_w, z2_s, z2_bf = [], [], []
+        for c, (lo, hi) in enumerate(TAPER):
+            part = sb.tile([P, PACK, hi - lo], F32, name="part%d" % c)
+            z2 = sb.tile([P, PACK, hi - lo], F32, name="z2_%d" % c)
+            for t in range(PACK):
+                nc.vector.tensor_tensor(part[:, t, :], b_win[t][:].indirect(entries(n3_t, lo, hi)), b_neg[t][:, lo:hi], ALU.add)
+                if t > 0:
+                    nc.vector.tensor_tensor(z2[:, t - 1, :], b_win[t - 1][:].indirect(entries(n4_t, lo, hi)), part[:, t - 1, :], ALU.add)
+            nc.vector.tensor_tensor(z2[:, 3, :], b_win[3][:].indirect(entries(n4_t, lo, hi)), part[:, 3, :], ALU.add)
+            if c == 0:
+                quantize(z_w[:], z_s[:], z_bf[:].rearrange("p u m t -> p (u m t)"))
+            else:
+                quantize(z2_w[c - 1][:], z2_s[c - 1][:], z2_bf[c - 1][:].rearrange("p c t -> p (c t)"))
+            last = c == len(TAPER) - 1
+            z2_bf.append(weave(nc.vector.tensor_copy if last else nc.scalar.copy, "z2_bf%d" % c, z2, hi - lo))
+            z2_w.append(sb.tile([P, hi - lo], U32, name="z2_w%d" % c, align_bytes=64))
+            z2_s.append(sb.tile([P, hi - lo], U8, name="z2_s%d" % c, align_bytes=64))
+        quantize(z2_w[-1][:], z2_s[-1][:], z2_bf[-1][:].rearrange("p c t -> p (c t)"))
+
+        s_ps = [bank(t, "s_ps%d" % t) for t in range(PACK)]
+        s_half, s_far, st2 = planes("s_half"), planes("s_far"), planes("st2")
+        for c, (lo, hi) in enumerate(TAPER):
+            for t in range(PACK):
+                nc.tensor.matmul_mx(
+                    out=s_ps[t][:, lo:hi],
+                    lhsT=z_w[:, P * t : P * (t + 1)].bitcast(FP8X4),
+                    lhsT_scale=z_s[:, P * t : P * (t + 1)],
+                    rhs=z2_w[c][:].bitcast(FP8X4),
+                    rhs_scale=z2_s[c][:],
+                    start=True,
+                    stop=True,
+                )
+            if c > 0:
+                first = 0 if c == 1 else lo
+                nc.scalar.activation(s_half[0][:, first:hi], s_ps[0][:, first:hi], ACT.Copy, scale=0.03125)
+        for t in range(1, PACK):
+            nc.scalar.activation(s_half[t][:], s_ps[t][:], ACT.Copy, scale=0.03125)
+
+        def larger(t):
+            nc.vector.scalar_tensor_tensor(st2[t][:], s_half[t][:], 2.0, s_far[t][:], ALU.mult, ALU.max)
+
+        for t in range(PACK):
+            for lo, hi in HALVES:
+                nc.vector.tensor_scalar(s_far[t][:, lo:hi], s_half[t][:].indirect(entries(n5_t, lo, hi)), 2.0, 0.0, ALU.mult, ALU.add)
+                if t > 0 and lo == 0:
+                    larger(t - 1)
+        larger(PACK - 1)
+
+        out_rows = out_0.rearrange("(p t) v -> p t v", t=PACK)
+        out_words = out_1[0].rearrange("p c r -> p (c r)").bitcast(I32)
+        y_s = sb.tile([P, N], U8, name="y_s", align_bytes=64)
+        y_bf = []
+
+        def hand_on(c):
+            lo, hi = TAPER[c]
+            y_w = sb.tile([P, hi - lo], I32, name="y_w%d" % c, align_bytes=64)
+            quantize(y_w[:], y_s[:, lo:hi], y_bf[c][:].rearrange("p c t -> p (c t)"))
+            nc.sync.dma_start(out_words[:, lo:hi], y_w[:])
+
+        for c, (lo, hi) in enumerate(TAPER):
+            y = sb.tile([P, PACK, hi - lo], F32, name="y%d" % c)
+            for t in range(PACK):
+                nc.vector.tensor_tensor(y[:, t, :], st2[t][:].indirect(entries(n6_t, lo, hi)), s_half[t][:, lo:hi], ALU.subtract)
+            nc.sync.dma_start(out_rows[:, :, lo:hi], y[:])
+            if c > 0:
+                hand_on(c - 1)
+            last = c == len(TAPER) - 1
+            y_bf.append(weave(nc.vector.tensor_copy if last else nc.scalar.copy, "y_bf%d" % c, y, hi - lo))
+        hand_on(len(TAPER) - 1)
+        for q in range(4):
+            queue = nc.scalar if q % 2 else nc.sync
+            queue.dma_start(out_2[0, 4 * q : 4 * q + 4, :].bitcast(I32), y_s[32 * q : 32 * q + 4, :].bitcast(I32))

@@ -18,6 +18,7 @@ P = 128
 T = 2048
 N = 512
 PACK = 4
+WHOLE = ((0, 512),)
 HALVES = ((0, 256), (256, 512))
 TAPER = ((0, 256), (256, 384), (384, 512))
 FLOPS = 3 * 2 * 512 * 512 * 512
@@ -48,12 +49,12 @@ def tile_picked_kqhopplaphopb_none_po_kernel(
             return ps.tile([P, N], F32, name=name, tag="bank%d" % k)
 
         xs = sb.tile([P, T], U8, name="xs")
-        w1s_raw = sb.tile([P, N], U8, name="w1s_raw")
+        w1s_raw = sb.tile([P, N], U8, name="w1s_raw", tag="w1s_then_xb", align_bytes=64)
         w2s_raw = sb.tile([P, N], U8, name="w2s_raw")
         g_rows = sb.tile([P, P], F32, name="g_rows")
-        nc.vector.memset(xs[:].bitcast(I32), 0)
+        nc.gpsimd.memset(xs[:].bitcast(I32), 0)
         nc.vector.memset(w1s_raw[:].bitcast(I32), 0)
-        nc.gpsimd.memset(w2s_raw[:].bitcast(I32), 0)
+        nc.vector.memset(w2s_raw[:].bitcast(I32), 0)
         nc.gpsimd.memset(g_rows[:], 0.0)
         ident = sb.tile([P, P], F32, name="ident")
         make_identity(nc, ident[:])
@@ -65,8 +66,8 @@ def tile_picked_kqhopplaphopb_none_po_kernel(
         nc.sync.dma_start(xw[:], x_words[0].rearrange("p n t -> p (n t)").bitcast(I32))
         w1w_raw = sb.tile([P, 256], I32, name="w1w_raw")
         w2w_raw = sb.tile([P, 256], I32, name="w2w_raw")
-        nc.scalar.dma_start(w1w_raw[:], w1_words[0].bitcast(I32))
-        load_scales(nc.scalar, w1s_raw, w1_scales)
+        nc.sync.dma_start(w1w_raw[:], w1_words[0].bitcast(I32))
+        load_scales(nc.sync, w1s_raw, w1_scales)
         n1_t = load_list("n1_t", n1)
         for r, g in ((0, ga), (4, gb)):
             nc.sync.dma_start(
@@ -99,18 +100,18 @@ def tile_picked_kqhopplaphopb_none_po_kernel(
             nc.vector.tensor_copy(tile[:], xs[:].indirect(lst[:]))
             return tile
 
-        def pick_words(name, lst):
-            tile = sb.tile([P, N], U32, name=name, align_bytes=64)
+        def pick_words(tag, lst):
+            tile = sb.tile([P, N], U32, name="picked_words", tag=tag, align_bytes=64)
             nc.vector.tensor_copy(tile[:], xw[:].bitcast(U32).indirect(lst[:]))
             return tile
 
-        def project(dst, w, t, words, scales):
+        def project(dst, w, t, words, scales, lo=0, hi=N):
             nc.tensor.matmul_mx(
-                out=dst[:],
+                out=dst[:, 0 : hi - lo],
                 lhsT=w[0][:, 256 * t : 256 * (t + 1)].bitcast(FP4X4),
                 lhsT_scale=w[1][:, P * t : P * (t + 1)],
-                rhs=words[:].bitcast(FP8X4),
-                rhs_scale=scales[:],
+                rhs=words[:, lo:hi].bitcast(FP8X4),
+                rhs_scale=scales[:, lo:hi],
                 start=True,
                 stop=True,
             )
@@ -119,43 +120,54 @@ def tile_picked_kqhopplaphopb_none_po_kernel(
         xb_s = pick_scales("xb_s", two_t)
         w1 = deal("w1", w1w_raw, w1s_raw)
         xa_w = pick_words("xa_w", offs_t)
-        xb_w = pick_words("xb_w", two_t)
-        w2 = deal("w2", w2w_raw, w2s_raw)
+        xb_w = pick_words("w1s_then_xb", two_t)
 
-        g_ps = bank(7, "g_ps")
+        def wide(name):
+            return [sb.tile([P, 2 * N], F32, name="%s%d" % (name, t)) for t in range(PACK)]
+
+        a_tile = [sb.tile([P, 2 * N if t else N], F32, name="a_tile%d" % t) for t in range(PACK)]
+        th_tile, b_tile, s_tile, st2_tile = wide("th_tile"), wide("b_tile"), wide("s_tile"), wide("st2_tile")
+        b_neg_last = sb.tile([P, N], F32, name="b_neg_last")
+        a_own = [tile[:, N:] for tile in a_tile[1:] + th_tile[:1]]
+        gs = [tile[:, N:] for tile in th_tile[1:] + b_tile[:1]]
+        b_neg = [tile[:, N:] for tile in b_tile[1:]] + [b_neg_last[:]]
+        st = [tile[:, N:] for tile in s_tile]
+        part = [tile[:, N:] for tile in st2_tile]
+
+        def fetch(dst, window, lst, other, op, lo=0, hi=N):
+            nc.vector.tensor_tensor(dst, window[:].indirect(entries(lst, lo, hi)), other[:, lo:hi], op)
+
+        for t in range(PACK):
+            pieces = WHOLE if t else HALVES
+            a_ps = {lo: bank(4 if lo else t, "a_ps%d_%d" % (t, lo)) for lo, hi in pieces}
+            for lo, hi in pieces:
+                project(a_ps[lo], w1, t, xa_w, xa_s, lo, hi)
+                nc.scalar.copy(a_tile[t][:, lo:hi], a_ps[lo][:, 0 : hi - lo])
+            for lo, hi in pieces:
+                nc.scalar.copy(a_own[t][:, lo:hi], a_ps[lo][:, 0 : hi - lo])
+                fetch(st[t][:, lo:hi], a_tile[t], n1_t, a_own[t], ALU.add, lo, hi)
+
+        g_ps = bank(4, "g_ps")
         nc.tensor.transpose(g_ps[:, 0:P], g_rows[:], ident[:])
         g_col = sb.tile([P, 12], F32, name="g_col")
         nc.scalar.activation(g_col[:, 0:4], g_ps[:, 0:4], ACT.Copy)
         nc.scalar.activation(g_col[:, 4:8], g_ps[:, 4:8], ACT.Copy, scale=0.75)
         nc.scalar.activation(g_col[:, 8:12], g_ps[:, 4:8], ACT.Copy, scale=-1.0)
 
-        def planes(name, width=N):
-            return [sb.tile([P, width], F32, name="%s%d" % (name, t)) for t in range(PACK)]
-
-        a_win, a_own, st, th, gs = planes("a_win"), planes("a_own"), planes("st"), planes("th"), planes("gs")
-        b_win, b_neg = planes("b_win"), planes("b_neg")
-
-        a_ps = [bank(t, "a_ps%d" % t) for t in range(PACK)]
-        for t in range(PACK):
-            project(a_ps[t], w1, t, xa_w, xa_s)
+        w2 = deal("w2", w2w_raw, w2s_raw)
         b_ps = [bank(4 + t, "b_ps%d" % t) for t in range(PACK)]
         for t in range(PACK):
             project(b_ps[t], w2, t, xb_w, xb_s)
 
-        for t in range(PACK):
-            nc.scalar.copy(a_win[t][:], a_ps[t][:])
-            nc.scalar.copy(a_own[t][:], a_ps[t][:])
-            for lo, hi in HALVES:
-                nc.vector.tensor_tensor(st[t][:, lo:hi], a_win[t][:].indirect(entries(n1_t, lo, hi)), a_own[t][:, lo:hi], ALU.add)
         z = sb.tile([P, PACK, N], F32, name="z")
         for t in range(PACK):
-            nc.scalar.activation(th[t][:], st[t][:], ACT.Tanh)
-            nc.scalar.activation(gs[t][:], st[t][:], ACT.Copy, scale=g_col[:, t : t + 1])
-            for lo, hi in HALVES:
-                nc.vector.tensor_tensor(z[:, t, lo:hi], th[t][:].indirect(entries(n2_t, lo, hi)), gs[t][:, lo:hi], ALU.mult)
+            nc.scalar.activation(th_tile[t][:, 0:N], st[t], ACT.Tanh)
+            nc.scalar.activation(gs[t], st[t], ACT.Copy, scale=g_col[:, t : t + 1])
+            fetch(z[:, t, :], th_tile[t], n2_t, gs[t], ALU.mult)
         for t in range(PACK):
-            nc.scalar.activation(b_win[t][:], b_ps[t][:], ACT.Copy, scale=g_col[:, 4 + t : 5 + t])
-            nc.scalar.activation(b_neg[t][:], b_ps[t][:], ACT.Copy, scale=g_col[:, 8 + t : 9 + t])
+            nc.scalar.activation(b_tile[t][:, 0:N], b_ps[t][:], ACT.Copy, scale=g_col[:, 4 + t : 5 + t])
+            nc.scalar.activation(b_neg[t], b_ps[t][:], ACT.Copy, scale=g_col[:, 8 + t : 9 + t])
+            fetch(part[t], b_tile[t], n3_t, b_neg[t], ALU.add)
 
         z_bf = sb.tile([P, PACK, P, PACK], BF16, name="z_bf", align_bytes=64)
         for lo, hi in HALVES:
@@ -163,86 +175,84 @@ def tile_picked_kqhopplaphopb_none_po_kernel(
                 z_bf[:, :, lo // 4 : hi // 4, :].rearrange("p u m t -> p m t u"),
                 z[:, :, lo:hi].rearrange("p t (m u) -> p m t u", u=4),
             )
-        z_w = sb.tile([P, N], U32, name="z_w", align_bytes=64)
-        z_s = sb.tile([P, N], U8, name="z_s", align_bytes=64)
 
-        def weave(engine_copy, name, src, width):
-            dst = sb.tile([P, width, PACK], BF16, name=name, align_bytes=64)
-            engine_copy(dst[:].rearrange("p (c i) t -> p c t i", i=4), src[:].rearrange("p t (c i) -> p c t i", i=4))
-            return dst
+        def weave(copy, name, src):
+            dst = sb.tile([P, src.shape[2], PACK], BF16, name=name, align_bytes=64)
+            copy(dst[:].rearrange("p (c i) t -> p c t i", i=4), src.rearrange("p t (c i) -> p c t i", i=4))
+            return dst[:].rearrange("p c t -> p (c t)")
+
+        def weave_half(name, src, h):
+            if h == 0:
+                return [weave(nc.scalar.copy, name + "0", src[:])]
+            return [weave(nc.vector.tensor_copy, name + "1", src[:, :, 0:P]), weave(nc.scalar.copy, name + "2", src[:, :, P:])]
 
         def quantize(words, scales, src):
             nc.vector.quantize_mx(out=words.bitcast(FP8X4), scales=scales, in_=src)
 
-        z2_w, z2_s, z2_bf = [], [], []
-        for c, (lo, hi) in enumerate(TAPER):
-            part = sb.tile([P, PACK, hi - lo], F32, name="part%d" % c)
-            z2 = sb.tile([P, PACK, hi - lo], F32, name="z2_%d" % c)
-            for t in range(PACK):
-                nc.vector.tensor_tensor(part[:, t, :], b_win[t][:].indirect(entries(n3_t, lo, hi)), b_neg[t][:, lo:hi], ALU.add)
-                if t > 0:
-                    nc.vector.tensor_tensor(z2[:, t - 1, :], b_win[t - 1][:].indirect(entries(n4_t, lo, hi)), part[:, t - 1, :], ALU.add)
-            nc.vector.tensor_tensor(z2[:, 3, :], b_win[3][:].indirect(entries(n4_t, lo, hi)), part[:, 3, :], ALU.add)
-            if c == 0:
-                quantize(z_w[:], z_s[:], z_bf[:].rearrange("p u m t -> p (u m t)"))
-            else:
-                quantize(z2_w[c - 1][:], z2_s[c - 1][:], z2_bf[c - 1][:].rearrange("p c t -> p (c t)"))
-            last = c == len(TAPER) - 1
-            z2_bf.append(weave(nc.vector.tensor_copy if last else nc.scalar.copy, "z2_bf%d" % c, z2, hi - lo))
-            z2_w.append(sb.tile([P, hi - lo], U32, name="z2_w%d" % c, align_bytes=64))
-            z2_s.append(sb.tile([P, hi - lo], U8, name="z2_s%d" % c, align_bytes=64))
-        quantize(z2_w[-1][:], z2_s[-1][:], z2_bf[-1][:].rearrange("p c t -> p (c t)"))
+        z_w = [sb.tile([P, P], U32, name="z_w%d" % u, align_bytes=64) for u in range(PACK)]
+        z_s = [sb.tile([P, P], U8, name="z_s%d" % u, align_bytes=64) for u in range(PACK)]
 
-        s_ps = [bank(t, "s_ps%d" % t) for t in range(PACK)]
-        s_half, s_far, st2 = planes("s_half"), planes("s_far"), planes("st2")
-        for c, (lo, hi) in enumerate(TAPER):
+        def quantize_z(u):
+            quantize(z_w[u][:], z_s[u][:], z_bf[:, u, :, :].rearrange("p m t -> p (m t)"))
+
+        z2_bf = []
+        for h, (lo, hi) in enumerate(HALVES):
+            z2 = sb.tile([P, PACK, hi - lo], F32, name="z2_%d" % h)
             for t in range(PACK):
+                fetch(z2[:, t, :], b_tile[t], n4_t, part[t], ALU.add, lo, hi)
+            z2_bf.extend(weave_half("z2_bf", z2, h))
+        quantize_z(0)
+        z2_w = [sb.tile([P, hi - lo], U32, name="z2_w%d" % lo, align_bytes=64) for lo, hi in TAPER]
+        z2_s = [sb.tile([P, hi - lo], U8, name="z2_s%d" % lo, align_bytes=64) for lo, hi in TAPER]
+        for c in range(len(TAPER)):
+            quantize(z2_w[c][:], z2_s[c][:], z2_bf[c])
+
+        s_half = [tile[:, 0:N] for tile in s_tile]
+        for t in range(PACK):
+            if t > 0:
+                quantize_z(t)
+            s_ps = bank(t, "s_ps%d" % t)
+            for c, (lo, hi) in enumerate(TAPER):
                 nc.tensor.matmul_mx(
-                    out=s_ps[t][:, lo:hi],
-                    lhsT=z_w[:, P * t : P * (t + 1)].bitcast(FP8X4),
-                    lhsT_scale=z_s[:, P * t : P * (t + 1)],
+                    out=s_ps[:, lo:hi],
+                    lhsT=z_w[t][:].bitcast(FP8X4),
+                    lhsT_scale=z_s[t][:],
                     rhs=z2_w[c][:].bitcast(FP8X4),
                     rhs_scale=z2_s[c][:],
                     start=True,
                     stop=True,
                 )
-            if c > 0:
-                first = 0 if c == 1 else lo
-                nc.scalar.activation(s_half[0][:, first:hi], s_ps[0][:, first:hi], ACT.Copy, scale=0.03125)
-        for t in range(1, PACK):
-            nc.scalar.activation(s_half[t][:], s_ps[t][:], ACT.Copy, scale=0.03125)
+                if t == 0 and c > 0:
+                    first = lo if c > 1 else 0
+                    nc.scalar.activation(s_half[t][:, first:hi], s_ps[:, first:hi], ACT.Copy, scale=0.03125)
+            if t > 0:
+                nc.scalar.activation(s_half[t], s_ps[:], ACT.Copy, scale=0.03125)
+
+        s_far = [sb.tile([P, N], F32, name="s_far%d" % t) for t in range(PACK)]
 
         def larger(t):
-            nc.vector.scalar_tensor_tensor(st2[t][:], s_half[t][:], 2.0, s_far[t][:], ALU.mult, ALU.max)
+            nc.vector.scalar_tensor_tensor(st2_tile[t][:, 0:N], s_half[t], 2.0, s_far[t][:], ALU.mult, ALU.max)
 
         for t in range(PACK):
-            for lo, hi in HALVES:
-                nc.vector.tensor_scalar(s_far[t][:, lo:hi], s_half[t][:].indirect(entries(n5_t, lo, hi)), 2.0, 0.0, ALU.mult, ALU.add)
-                if t > 0 and lo == 0:
-                    larger(t - 1)
+            nc.vector.tensor_scalar(s_far[t][:], s_tile[t][:].indirect(n5_t[:]), 2.0, 0.0, ALU.mult, ALU.add)
+            if t > 0:
+                larger(t - 1)
         larger(PACK - 1)
 
         out_rows = out_0.rearrange("(p t) v -> p t v", t=PACK)
         out_words = out_1[0].rearrange("p c r -> p (c r)").bitcast(I32)
         y_s = sb.tile([P, N], U8, name="y_s", align_bytes=64)
         y_bf = []
-
-        def hand_on(c):
-            lo, hi = TAPER[c]
-            y_w = sb.tile([P, hi - lo], I32, name="y_w%d" % c, align_bytes=64)
-            quantize(y_w[:], y_s[:, lo:hi], y_bf[c][:].rearrange("p c t -> p (c t)"))
-            nc.sync.dma_start(out_words[:, lo:hi], y_w[:])
-
-        for c, (lo, hi) in enumerate(TAPER):
-            y = sb.tile([P, PACK, hi - lo], F32, name="y%d" % c)
+        for h, (lo, hi) in enumerate(HALVES):
+            y = sb.tile([P, PACK, hi - lo], F32, name="y%d" % h)
             for t in range(PACK):
-                nc.vector.tensor_tensor(y[:, t, :], st2[t][:].indirect(entries(n6_t, lo, hi)), s_half[t][:, lo:hi], ALU.subtract)
+                fetch(y[:, t, :], st2_tile[t], n6_t, s_half[t], ALU.subtract, lo, hi)
             nc.sync.dma_start(out_rows[:, :, lo:hi], y[:])
-            if c > 0:
-                hand_on(c - 1)
-            last = c == len(TAPER) - 1
-            y_bf.append(weave(nc.vector.tensor_copy if last else nc.scalar.copy, "y_bf%d" % c, y, hi - lo))
-        hand_on(len(TAPER) - 1)
+            y_bf.extend(weave_half("y_bf", y, h))
+        y_w = sb.tile([P, N], I32, name="y_w", align_bytes=64)
+        for c, (lo, hi) in enumerate(TAPER):
+            quantize(y_w[:, lo:hi], y_s[:, lo:hi], y_bf[c])
+        nc.sync.dma_start(out_words, y_w[:])
         for q in range(4):
             queue = nc.scalar if q % 2 else nc.sync
             queue.dma_start(out_2[0, 4 * q : 4 * q + 4, :].bitcast(I32), y_s[32 * q : 32 * q + 4, :].bitcast(I32))

@@ -18,6 +18,7 @@ P = 128
 T = 2048
 N = 512
 PACK = 4
+TURNED = 1
 WHOLE = ((0, 512),)
 HALVES = ((0, 256), (256, 512))
 TAPER = ((0, 256), (256, 384), (384, 512))
@@ -61,12 +62,12 @@ def tile_picked_kqhopplaphopb_none_po_kernel(
 
         offs_t = load_list("offs_t", offs)
         two_t = load_list("two_t", two)
-        load_scales(nc.sync, xs, x_scales)
-        xw = sb.tile([P, T], I32, name="xw")
-        nc.sync.dma_start(xw[:], x_words[0].rearrange("p n t -> p (n t)").bitcast(I32))
         w1w_raw = sb.tile([P, 256], I32, name="w1w_raw")
         w2w_raw = sb.tile([P, 256], I32, name="w2w_raw")
         nc.sync.dma_start(w1w_raw[:], w1_words[0].bitcast(I32))
+        load_scales(nc.sync, xs, x_scales)
+        xw = sb.tile([P, T], I32, name="xw")
+        nc.sync.dma_start(xw[:], x_words[0].rearrange("p n t -> p (n t)").bitcast(I32))
         load_scales(nc.sync, w1s_raw, w1_scales)
         n1_t = load_list("n1_t", n1)
         for r, g in ((0, ga), (4, gb)):
@@ -127,7 +128,7 @@ def tile_picked_kqhopplaphopb_none_po_kernel(
 
         a_tile = [sb.tile([P, 2 * N if t else N], F32, name="a_tile%d" % t) for t in range(PACK)]
         th_tile, b_tile, s_tile, st2_tile = wide("th_tile"), wide("b_tile"), wide("s_tile"), wide("st2_tile")
-        b_neg_last = sb.tile([P, N], F32, name="b_neg_last")
+        b_neg_last = sb.tile([P, N], F32, name="b_neg_last", tag="b_neg_then_z2", align_bytes=64)
         a_own = [tile[:, N:] for tile in a_tile[1:] + th_tile[:1]]
         gs = [tile[:, N:] for tile in th_tile[1:] + b_tile[:1]]
         b_neg = [tile[:, N:] for tile in b_tile[1:]] + [b_neg_last[:]]
@@ -169,87 +170,111 @@ def tile_picked_kqhopplaphopb_none_po_kernel(
             nc.scalar.activation(b_neg[t], b_ps[t][:], ACT.Copy, scale=g_col[:, 8 + t : 9 + t])
             fetch(part[t], b_tile[t], n3_t, b_neg[t], ALU.add)
 
-        z_bf = sb.tile([P, PACK, P, PACK], BF16, name="z_bf", align_bytes=64)
-        for lo, hi in HALVES:
-            nc.scalar.copy(
-                z_bf[:, :, lo // 4 : hi // 4, :].rearrange("p u m t -> p m t u"),
-                z[:, :, lo:hi].rearrange("p t (m u) -> p m t u", u=4),
-            )
+        z_bf_first = sb.tile([P, P, PACK], BF16, name="z_bf_first", tag="z_bf_then_z2", align_bytes=64)
+        z_bf_rest = sb.tile([P, PACK - 1, P, PACK], BF16, name="z_bf_rest", align_bytes=64)
+        z_by_class = z[:].rearrange("p t (m u) -> p m t u", u=PACK)
+        nc.scalar.copy(z_bf_first[:], z_by_class[:, :, :, 0])
+        nc.scalar.copy(z_bf_rest[:].rearrange("p u m t -> p m t u"), z_by_class[:, :, :, 1:])
 
-        def weave(copy, name, src):
-            dst = sb.tile([P, src.shape[2], PACK], BF16, name=name, align_bytes=64)
+        def weave(copy, name, src, tag):
+            dst = sb.tile([P, src.shape[2], PACK], BF16, name=name, tag=tag, align_bytes=64)
             copy(dst[:].rearrange("p (c i) t -> p c t i", i=4), src.rearrange("p t (c i) -> p c t i", i=4))
             return dst[:].rearrange("p c t -> p (c t)")
 
         def weave_half(name, src, h):
             if h == 0:
-                return [weave(nc.scalar.copy, name + "0", src[:])]
-            return [weave(nc.vector.tensor_copy, name + "1", src[:, :, 0:P]), weave(nc.scalar.copy, name + "2", src[:, :, P:])]
+                return [weave(nc.scalar.copy, name, src[:], name + "0")]
+            return [weave(nc.vector.tensor_copy, name, src[:, :, 0:P], name + "1"), weave(nc.scalar.copy, name, src[:, :, P:], name + "2")]
 
         def quantize(words, scales, src):
             nc.vector.quantize_mx(out=words.bitcast(FP8X4), scales=scales, in_=src)
 
-        z_w = [sb.tile([P, P], U32, name="z_w%d" % u, align_bytes=64) for u in range(PACK)]
-        z_s = [sb.tile([P, P], U8, name="z_s%d" % u, align_bytes=64) for u in range(PACK)]
-
-        def quantize_z(u):
-            quantize(z_w[u][:], z_s[u][:], z_bf[:, u, :, :].rearrange("p m t -> p (m t)"))
-
+        z_w_first = sb.tile([P, P], U32, name="z_w_first", align_bytes=64)
+        z_s = sb.tile([P, N], U8, name="z_s", align_bytes=64)
         z2_bf = []
         for h, (lo, hi) in enumerate(HALVES):
-            z2 = sb.tile([P, PACK, hi - lo], F32, name="z2_%d" % h)
+            if h == 1:
+                quantize(z_w_first[:], z_s[:, 0:P], z_bf_first[:].rearrange("p m t -> p (m t)"))
+            z2 = sb.tile([P, PACK, hi - lo], F32, name="z2", tag=("b_neg_then_z2", "z_bf_then_z2")[h], align_bytes=64)
             for t in range(PACK):
                 fetch(z2[:, t, :], b_tile[t], n4_t, part[t], ALU.add, lo, hi)
             z2_bf.extend(weave_half("z2_bf", z2, h))
-        quantize_z(0)
-        z2_w = [sb.tile([P, hi - lo], U32, name="z2_w%d" % lo, align_bytes=64) for lo, hi in TAPER]
-        z2_s = [sb.tile([P, hi - lo], U8, name="z2_s%d" % lo, align_bytes=64) for lo, hi in TAPER]
-        for c in range(len(TAPER)):
-            quantize(z2_w[c][:], z2_s[c][:], z2_bf[c])
+        z2_w = sb.tile([P, N], U32, name="z2_w", align_bytes=64)
+        z2_s = sb.tile([P, N], U8, name="z2_s", align_bytes=64)
+        for c, (lo, hi) in enumerate(TAPER):
+            quantize(z2_w[:, lo:hi], z2_s[:, lo:hi], z2_bf[c])
+        z_w_rest = sb.tile([P, (PACK - 1) * P], U32, name="z_w_rest", tag="z2_bf2", align_bytes=64)
+        z_w = [z_w_first[:]] + [z_w_rest[:, P * u : P * (u + 1)] for u in range(PACK - 1)]
 
-        s_half = [tile[:, 0:N] for tile in s_tile]
+        s_neg = [tile[:, 0:N] for tile in s_tile]
         for t in range(PACK):
             if t > 0:
-                quantize_z(t)
+                quantize(z_w[t], z_s[:, P * t : P * (t + 1)], z_bf_rest[:, t - 1, :, :].rearrange("p m t -> p (m t)"))
             s_ps = bank(t, "s_ps%d" % t)
-            for c, (lo, hi) in enumerate(TAPER):
+            for c, (lo, hi) in enumerate(WHOLE if t else TAPER):
                 nc.tensor.matmul_mx(
                     out=s_ps[:, lo:hi],
-                    lhsT=z_w[t][:].bitcast(FP8X4),
-                    lhsT_scale=z_s[t][:],
-                    rhs=z2_w[c][:].bitcast(FP8X4),
-                    rhs_scale=z2_s[c][:],
+                    lhsT=z_w[t].bitcast(FP8X4),
+                    lhsT_scale=z_s[:, P * t : P * (t + 1)],
+                    rhs=z2_w[:, lo:hi].bitcast(FP8X4),
+                    rhs_scale=z2_s[:, lo:hi],
                     start=True,
                     stop=True,
                 )
                 if t == 0 and c > 0:
                     first = lo if c > 1 else 0
-                    nc.scalar.activation(s_half[t][:, first:hi], s_ps[:, first:hi], ACT.Copy, scale=0.03125)
+                    nc.scalar.activation(s_neg[t][:, first:hi], s_ps[:, first:hi], ACT.Copy, scale=-0.03125)
             if t > 0:
-                nc.scalar.activation(s_half[t], s_ps[:], ACT.Copy, scale=0.03125)
+                nc.scalar.activation(s_neg[t], s_ps[:], ACT.Copy, scale=-0.03125)
 
         s_far = [sb.tile([P, N], F32, name="s_far%d" % t) for t in range(PACK)]
 
-        def larger(t):
-            nc.vector.scalar_tensor_tensor(st2_tile[t][:, 0:N], s_half[t], 2.0, s_far[t][:], ALU.mult, ALU.max)
+        def block(k):
+            return slice(P * k, P * (k + 1))
 
+        def turn(dst, *terms):
+            for k in range(PACK):
+                for j, term in enumerate(terms):
+                    nc.tensor.matmul(dst[:, block(k)], term[:, block(k)], ident[:], start=(j == 0), stop=(j == len(terms) - 1), is_transpose=True)
+
+        def larger_by_vector(t):
+            nc.vector.scalar_tensor_tensor(st2_tile[t][:, 0:N], s_neg[t], -2.0, s_far[t][:], ALU.mult, ALU.max)
+
+        own = [sb.tile([P, N], F32, name="own%d" % t) for t in range(TURNED)]
+        gap = [sb.tile([P, N], F32, name="gap", tag="gap%d" % t) for t in range(TURNED)]
+        for t in range(TURNED):
+            own_ps = bank(4 + t % 2, "own_ps%d" % t)
+            turn(own_ps, s_neg[t])
+            nc.scalar.activation(own[t][:], own_ps[:], ACT.Copy, scale=-2.0)
         for t in range(PACK):
-            nc.vector.tensor_scalar(s_far[t][:], s_tile[t][:].indirect(n5_t[:]), 2.0, 0.0, ALU.mult, ALU.add)
-            if t > 0:
-                larger(t - 1)
-        larger(PACK - 1)
+            factor = -1.0 if t < TURNED else -2.0
+            nc.vector.tensor_scalar(s_far[t][:], s_tile[t][:].indirect(n5_t[:]), factor, 0.0, ALU.mult, ALU.add)
+            if t > TURNED:
+                larger_by_vector(t - 1)
+        larger_by_vector(PACK - 1)
+        for t in range(TURNED):
+            gap_ps = bank(6 + t % 2, "gap_ps%d" % t)
+            turn(gap_ps, s_neg[t], s_far[t])
+            nc.scalar.activation(gap[t][:], gap_ps[:], ACT.Relu, scale=2.0)
+        for t in range(TURNED):
+            st2_ps = bank(t, "st2_ps%d" % t)
+            turn(st2_ps, own[t], gap[t])
+            nc.scalar.copy(st2_tile[t][:, 0:N], st2_ps[:])
 
         out_rows = out_0.rearrange("(p t) v -> p t v", t=PACK)
         out_words = out_1[0].rearrange("p c r -> p (c r)").bitcast(I32)
         y_s = sb.tile([P, N], U8, name="y_s", align_bytes=64)
+        y_w = sb.tile([P, N], I32, name="y_w", align_bytes=64)
         y_bf = []
         for h, (lo, hi) in enumerate(HALVES):
-            y = sb.tile([P, PACK, hi - lo], F32, name="y%d" % h)
-            for t in range(PACK):
-                fetch(y[:, t, :], st2_tile[t], n6_t, s_half[t], ALU.subtract, lo, hi)
-            nc.sync.dma_start(out_rows[:, :, lo:hi], y[:])
+            y = sb.tile([P, PACK, hi - lo], F32, name="y", tag="gap%d" % (TURNED - 1) if h else "y0")
+            for t in list(range(TURNED, PACK)) + list(range(TURNED)):
+                fetch(y[:, t, :], st2_tile[t], n6_t, s_neg[t], ALU.add, lo, hi)
+                if h == 1:
+                    nc.sync.dma_start(out_rows[:, t, lo:hi], y[:, t, :])
+            if h == 0:
+                nc.sync.dma_start(out_rows[:, :, lo:hi], y[:])
             y_bf.extend(weave_half("y_bf", y, h))
-        y_w = sb.tile([P, N], I32, name="y_w", align_bytes=64)
         for c, (lo, hi) in enumerate(TAPER):
             quantize(y_w[:, lo:hi], y_s[:, lo:hi], y_bf[c])
         nc.sync.dma_start(out_words, y_w[:])

from contextlib import ExitStack

import concourse.mybir as mybir
from concourse.masks import make_identity

F32 = mybir.dt.float32
BF16 = mybir.dt.bfloat16
I32 = mybir.dt.int32
U32 = mybir.dt.uint32
U16 = mybir.dt.uint16
U8 = mybir.dt.uint8
FP8X4 = mybir.dt.float8_e4m3fn_x4
FP4X4 = mybir.dt.float4_e2m1fn_x4
ALU = mybir.AluOpType
ACT = mybir.ActivationFunctionType

P = 128
T = 2048
N = 512
PACK = 4
TURNED = 1
WHOLE = ((0, 512),)
HALVES = ((0, 256), (256, 512))
TAPER = ((0, 256), (256, 384), (384, 512))
FLOPS = 3 * 2 * 512 * 512 * 512


def tile_picked_kqhopplaphopb_none_po_kernel(
    tc, x_words, x_scales, w1_words, w1_scales, w2_words, w2_scales, ga, gb, offs, two, n1, n2, n3, n4, n5, n6, out_0, out_1, out_2
):
    nc = tc.nc
    with ExitStack() as ctx:
        lists = ctx.enter_context(tc.tile_pool(name="lists", bufs=1))
        sb = ctx.enter_context(tc.tile_pool(name="sb", bufs=1))
        ps = ctx.enter_context(tc.psum_pool(name="ps", bufs=1))

        def load_list(name, src):
            tile = lists.tile([P, N // 16], U16, name=name)
            nc.sync.dma_start(tile[:], src)
            return tile

        def entries(tile, lo, hi):
            return tile[:, lo // 16 : hi // 16]

        def load_scales(queue, tile, src):
            for q in range(4):
                queue.dma_start(tile[32 * q : 32 * q + 4, :].bitcast(I32), src[0, 4 * q : 4 * q + 4, :].bitcast(I32))

        def bank(k, name):
            return ps.tile([P, N], F32, name=name, tag="bank%d" % k)

        xs = sb.tile([P, T], U8, name="xs")
        w1s_raw = sb.tile([P, N], U8, name="w1s_raw", tag="w1s_then_xb", align_bytes=64)
        w2s_raw = sb.tile([P, N], U8, name="w2s_raw")
        g_rows = sb.tile([P, P], F32, name="g_rows")
        nc.gpsimd.memset(xs[:].bitcast(I32), 0)
        nc.vector.memset(w1s_raw[:].bitcast(I32), 0)
        nc.vector.memset(w2s_raw[:].bitcast(I32), 0)
        nc.gpsimd.memset(g_rows[:], 0.0)
        ident = sb.tile([P, P], F32, name="ident")
        make_identity(nc, ident[:])

        offs_t = load_list("offs_t", offs)
        two_t = load_list("two_t", two)
        w1w_raw = sb.tile([P, 256], I32, name="w1w_raw")
        w2w_raw = sb.tile([P, 256], I32, name="w2w_raw")
        nc.sync.dma_start(w1w_raw[:], w1_words[0].bitcast(I32))
        load_scales(nc.sync, xs, x_scales)
        xw = sb.tile([P, T], I32, name="xw")
        nc.sync.dma_start(xw[:], x_words[0].rearrange("p n t -> p (n t)").bitcast(I32))
        load_scales(nc.sync, w1s_raw, w1_scales)
        n1_t = load_list("n1_t", n1)
        for r, g in ((0, ga), (4, gb)):
            nc.sync.dma_start(
                g_rows[r : r + 4, :].rearrange("t (b q) -> t b q", q=8),
                g.rearrange("(b t q) o -> t b (q o)", t=4, q=8),
            )
        nc.sync.dma_start(w2w_raw[:], w2_words[0].bitcast(I32))
        load_scales(nc.sync, w2s_raw, w2_scales)
        n2_t = load_list("n2_t", n2)
        n3_t = load_list("n3_t", n3)
        n4_t = load_list("n4_t", n4)
        n5_t = load_list("n5_t", n5)
        n6_t = load_list("n6_t", n6)

        def deal(name, words_raw, scales_raw):
            words = sb.tile([P, 2 * N], U8, name=name + "w", align_bytes=64)
            scales = sb.tile([P, N], U8, name=name + "s", align_bytes=64)
            nc.vector.tensor_copy(
                words[:].bitcast(I32).rearrange("p (t b q) -> p t b q", t=4, q=4),
                words_raw[:].rearrange("p (b t q) -> p t b q", t=4, q=4),
            )
            nc.vector.tensor_copy(
                scales[:].bitcast(I32).rearrange("p (t b q) -> p t b q", t=4, q=2),
                scales_raw[:].bitcast(I32).rearrange("p (b t q) -> p t b q", t=4, q=2),
            )
            return words, scales

        def pick_scales(name, lst):
            tile = sb.tile([P, N], U8, name=name, align_bytes=64)
            nc.vector.tensor_copy(tile[:], xs[:].indirect(lst[:]))
            return tile

        def pick_words(tag, lst):
            tile = sb.tile([P, N], U32, name="picked_words", tag=tag, align_bytes=64)
            nc.vector.tensor_copy(tile[:], xw[:].bitcast(U32).indirect(lst[:]))
            return tile

        def project(dst, w, t, words, scales, lo=0, hi=N):
            nc.tensor.matmul_mx(
                out=dst[:, 0 : hi - lo],
                lhsT=w[0][:, 256 * t : 256 * (t + 1)].bitcast(FP4X4),
                lhsT_scale=w[1][:, P * t : P * (t + 1)],
                rhs=words[:, lo:hi].bitcast(FP8X4),
                rhs_scale=scales[:, lo:hi],
                start=True,
                stop=True,
            )

        xa_s = pick_scales("xa_s", offs_t)
        xb_s = pick_scales("xb_s", two_t)
        w1 = deal("w1", w1w_raw, w1s_raw)
        xa_w = pick_words("xa_w", offs_t)
        xb_w = pick_words("w1s_then_xb", two_t)

        def wide(name):
            return [sb.tile([P, 2 * N], F32, name="%s%d" % (name, t)) for t in range(PACK)]

        a_tile = [sb.tile([P, 2 * N if t else N], F32, name="a_tile%d" % t) for t in range(PACK)]
        th_tile, b_tile, s_tile, st2_tile = wide("th_tile"), wide("b_tile"), wide("s_tile"), wide("st2_tile")
        b_neg_last = sb.tile([P, N], F32, name="b_neg_last", tag="b_neg_then_z2", align_bytes=64)
        a_own = [tile[:, N:] for tile in a_tile[1:] + th_tile[:1]]
        gs = [tile[:, N:] for tile in th_tile[1:] + b_tile[:1]]
        b_neg = [tile[:, N:] for tile in b_tile[1:]] + [b_neg_last[:]]
        st = [tile[:, N:] for tile in s_tile]
        part = [tile[:, N:] for tile in st2_tile]

        def fetch(dst, window, lst, other, op, lo=0, hi=N):
            nc.vector.tensor_tensor(dst, window[:].indirect(entries(lst, lo, hi)), other[:, lo:hi], op)

        for t in range(PACK):
            pieces = WHOLE if t else HALVES
            a_ps = {lo: bank(4 if lo else t, "a_ps%d_%d" % (t, lo)) for lo, hi in pieces}
            for lo, hi in pieces:
                project(a_ps[lo], w1, t, xa_w, xa_s, lo, hi)
                nc.scalar.copy(a_tile[t][:, lo:hi], a_ps[lo][:, 0 : hi - lo])
            for lo, hi in pieces:
                nc.scalar.copy(a_own[t][:, lo:hi], a_ps[lo][:, 0 : hi - lo])
                fetch(st[t][:, lo:hi], a_tile[t], n1_t, a_own[t], ALU.add, lo, hi)

        g_ps = bank(4, "g_ps")
        nc.tensor.transpose(g_ps[:, 0:P], g_rows[:], ident[:])
        g_col = sb.tile([P, 12], F32, name="g_col")
        nc.scalar.activation(g_col[:, 0:4], g_ps[:, 0:4], ACT.Copy)
        nc.scalar.activation(g_col[:, 4:8], g_ps[:, 4:8], ACT.Copy, scale=0.75)
        nc.scalar.activation(g_col[:, 8:12], g_ps[:, 4:8], ACT.Copy, scale=-1.0)

        w2 = deal("w2", w2w_raw, w2s_raw)
        b_ps = [bank(4 + t, "b_ps%d" % t) for t in range(PACK)]
        for t in range(PACK):
            project(b_ps[t], w2, t, xb_w, xb_s)

        z = sb.tile([P, PACK, N], F32, name="z")
        for t in range(PACK):
            nc.scalar.activation(th_tile[t][:, 0:N], st[t], ACT.Tanh)
            nc.scalar.activation(gs[t], st[t], ACT.Copy, scale=g_col[:, t : t + 1])
            fetch(z[:, t, :], th_tile[t], n2_t, gs[t], ALU.mult)
        for t in range(PACK):
            nc.scalar.activation(b_tile[t][:, 0:N], b_ps[t][:], ACT.Copy, scale=g_col[:, 4 + t : 5 + t])
            nc.scalar.activation(b_neg[t], b_ps[t][:], ACT.Copy, scale=g_col[:, 8 + t : 9 + t])
            fetch(part[t], b_tile[t], n3_t, b_neg[t], ALU.add)

        z_bf_first = sb.tile([P, P, PACK], BF16, name="z_bf_first", tag="z_bf_then_z2", align_bytes=64)
        z_bf_rest = sb.tile([P, PACK - 1, P, PACK], BF16, name="z_bf_rest", align_bytes=64)
        z_by_class = z[:].rearrange("p t (m u) -> p m t u", u=PACK)
        nc.scalar.copy(z_bf_first[:], z_by_class[:, :, :, 0])
        nc.scalar.copy(z_bf_rest[:].rearrange("p u m t -> p m t u"), z_by_class[:, :, :, 1:])

        def weave(copy, name, src, tag):
            dst = sb.tile([P, src.shape[2], PACK], BF16, name=name, tag=tag, align_bytes=64)
            copy(dst[:].rearrange("p (c i) t -> p c t i", i=4), src.rearrange("p t (c i) -> p c t i", i=4))
            return dst[:].rearrange("p c t -> p (c t)")

        def weave_half(name, src, h):
            if h == 0:
                return [weave(nc.scalar.copy, name, src[:], name + "0")]
            return [weave(nc.vector.tensor_copy, name, src[:, :, 0:P], name + "1"), weave(nc.scalar.copy, name, src[:, :, P:], name + "2")]

        def quantize(words, scales, src):
            nc.vector.quantize_mx(out=words.bitcast(FP8X4), scales=scales, in_=src)

        z_w_first = sb.tile([P, P], U32, name="z_w_first", align_bytes=64)
        z_s = sb.tile([P, N], U8, name="z_s", align_bytes=64)
        z2_bf = []
        for h, (lo, hi) in enumerate(HALVES):
            if h == 1:
                quantize(z_w_first[:], z_s[:, 0:P], z_bf_first[:].rearrange("p m t -> p (m t)"))
            z2 = sb.tile([P, PACK, hi - lo], F32, name="z2", tag=("b_neg_then_z2", "z_bf_then_z2")[h], align_bytes=64)
            for t in range(PACK):
                fetch(z2[:, t, :], b_tile[t], n4_t, part[t], ALU.add, lo, hi)
            z2_bf.extend(weave_half("z2_bf", z2, h))
        z2_w = sb.tile([P, N], U32, name="z2_w", align_bytes=64)
        z2_s = sb.tile([P, N], U8, name="z2_s", align_bytes=64)
        for c, (lo, hi) in enumerate(TAPER):
            quantize(z2_w[:, lo:hi], z2_s[:, lo:hi], z2_bf[c])
        z_w_rest = sb.tile([P, (PACK - 1) * P], U32, name="z_w_rest", tag="z2_bf2", align_bytes=64)
        z_w = [z_w_first[:]] + [z_w_rest[:, P * u : P * (u + 1)] for u in range(PACK - 1)]

        s_neg = [tile[:, 0:N] for tile in s_tile]
        for t in range(PACK):
            if t > 0:
                quantize(z_w[t], z_s[:, P * t : P * (t + 1)], z_bf_rest[:, t - 1, :, :].rearrange("p m t -> p (m t)"))
            s_ps = bank(t, "s_ps%d" % t)
            for c, (lo, hi) in enumerate(WHOLE if t else TAPER):
                nc.tensor.matmul_mx(
                    out=s_ps[:, lo:hi],
                    lhsT=z_w[t].bitcast(FP8X4),
                    lhsT_scale=z_s[:, P * t : P * (t + 1)],
                    rhs=z2_w[:, lo:hi].bitcast(FP8X4),
                    rhs_scale=z2_s[:, lo:hi],
                    start=True,
                    stop=True,
                )
                if t == 0 and c > 0:
                    first = lo if c > 1 else 0
                    nc.scalar.activation(s_neg[t][:, first:hi], s_ps[:, first:hi], ACT.Copy, scale=-0.03125)
            if t > 0:
                nc.scalar.activation(s_neg[t], s_ps[:], ACT.Copy, scale=-0.03125)

        s_far = [sb.tile([P, N], F32, name="s_far%d" % t) for t in range(PACK)]

        def block(k):
            return slice(P * k, P * (k + 1))

        def turn(dst, *terms):
            for k in range(PACK):
                for j, term in enumerate(terms):
                    nc.tensor.matmul(dst[:, block(k)], term[:, block(k)], ident[:], start=(j == 0), stop=(j == len(terms) - 1), is_transpose=True)

        def larger_by_vector(t):
            nc.vector.scalar_tensor_tensor(st2_tile[t][:, 0:N], s_neg[t], -2.0, s_far[t][:], ALU.mult, ALU.max)

        own = [sb.tile([P, N], F32, name="own%d" % t) for t in range(TURNED)]
        gap = [sb.tile([P, N], F32, name="gap", tag="gap%d" % t) for t in range(TURNED)]
        for t in range(TURNED):
            own_ps = bank(4 + t % 2, "own_ps%d" % t)
            turn(own_ps, s_neg[t])
            nc.scalar.activation(own[t][:], own_ps[:], ACT.Copy, scale=-2.0)
        for t in range(PACK):
            factor = -1.0 if t < TURNED else -2.0
            nc.vector.tensor_scalar(s_far[t][:], s_tile[t][:].indirect(n5_t[:]), factor, 0.0, ALU.mult, ALU.add)
            if t > TURNED:
                larger_by_vector(t - 1)
        larger_by_vector(PACK - 1)
        for t in range(TURNED):
            gap_ps = bank(6 + t % 2, "gap_ps%d" % t)
            turn(gap_ps, s_neg[t], s_far[t])
            nc.scalar.activation(gap[t][:], gap_ps[:], ACT.Relu, scale=2.0)
        for t in range(TURNED):
            st2_ps = bank(t, "st2_ps%d" % t)
            turn(st2_ps, own[t], gap[t])
            nc.scalar.copy(st2_tile[t][:, 0:N], st2_ps[:])

        out_rows = out_0.rearrange("(p t) v -> p t v", t=PACK)
        out_words = out_1[0].rearrange("p c r -> p (c r)").bitcast(I32)
        y_s = sb.tile([P, N], U8, name="y_s", align_bytes=64)
        y_w = sb.tile([P, N], I32, name="y_w", align_bytes=64)
        y_bf = []
        for h, (lo, hi) in enumerate(HALVES):
            y = sb.tile([P, PACK, hi - lo], F32, name="y", tag="gap%d" % (TURNED - 1) if h else "y0")
            for t in list(range(TURNED, PACK)) + list(range(TURNED)):
                fetch(y[:, t, :], st2_tile[t], n6_t, s_neg[t], ALU.add, lo, hi)
                if h == 1:
                    nc.sync.dma_start(out_rows[:, t, lo:hi], y[:, t, :])
            if h == 0:
                nc.sync.dma_start(out_rows[:, :, lo:hi], y[:])
            y_bf.extend(weave_half("y_bf", y, h))
        for c, (lo, hi) in enumerate(TAPER):
            quantize(y_w[:, lo:hi], y_s[:, lo:hi], y_bf[c])
        nc.sync.dma_start(out_words, y_w[:])
        for q in range(4):
            queue = nc.scalar if q % 2 else nc.sync
            queue.dma_start(out_2[0, 4 * q : 4 * q + 4, :].bitcast(I32), y_s[32 * q : 32 * q + 4, :].bitcast(I32))
